import numpy as np
import ml_dtypes


def mxq(x, axis, fmt="e4m3"):
    dtype, down = {"e4m3": (ml_dtypes.float8_e4m3fn, 7), "e5m2": (ml_dtypes.float8_e5m2, 14)}[fmt]
    v = np.moveaxis(np.asarray(x, np.float32).astype(ml_dtypes.bfloat16).astype(np.float64), axis, -1)
    blocks = v.reshape(v.shape[:-1] + (-1, 32))
    amax = np.abs(blocks).max(-1, keepdims=True)
    byte = np.maximum(np.where(amax > 0, np.frexp(amax)[1] - 1 + 127, 0) - down, 1)
    scale = np.exp2(byte - 127.0)
    codes = (blocks / scale).astype(np.float32).astype(dtype).astype(np.float64)
    return np.moveaxis((codes * scale).reshape(v.shape), -1, axis)


WIDE = False


def mx_kscale(k):
    if not WIDE:
        return np.ones(k)
    levels = np.array([10, -10, 5, -5, 0])
    if k % 512:
        return np.exp2(np.random.permutation(np.resize(levels, k // 32))).repeat(32)
    a = np.empty((k // 512, 16))
    for p in range(k // 512):
        a[p, :8] = np.random.permutation(np.resize(levels, 8))
        for g in range(8):
            far = levels[np.abs(levels - a[p, g]) >= 10]
            a[p, g + 8] = far[np.random.randint(len(far))]
    return np.exp2(a.ravel()).repeat(32)


BF16 = ml_dtypes.bfloat16


def bf(x):
    return np.asarray(x, np.float32).astype(BF16)


def f64(x):
    return np.asarray(x).astype(np.float64)


E2M1 = np.array([0.0, 0.5, 1.0, 1.5, 2.0, 3.0, 4.0, 6.0, -0.0, -0.5, -1.0, -1.5, -2.0, -3.0, -4.0, -6.0])


def pack_weight(w, fmt):
    k, n = w.shape
    w = f64(bf(w)).reshape(k // 32, 32, n)
    amax = np.abs(w).max(1)
    if fmt == "e4m3":
        byte = np.frexp(amax)[1] - 1 + 127 - 7
    else:
        mant, ex = np.frexp(amax / 6.0)
        byte = np.where(mant > 0.5, ex, ex - 1) + 127
    byte = np.clip(np.where(amax > 0, byte, 1), 1, 254)
    scaled = (w * np.exp2(127.0 - byte)[:, None, :]).reshape(k, n).astype(np.float32)
    by_word = np.ascontiguousarray(scaled.reshape(k // 512, 128, 4, n).transpose(0, 1, 3, 2))
    if fmt == "e4m3":
        words = by_word.astype(ml_dtypes.float8_e4m3fn).view(np.uint8)
    else:
        c = by_word.astype(ml_dtypes.float4_e2m1fn).view(np.uint8) & 0xF
        words = c[..., 0::2] | (c[..., 1::2] << 4)
    return np.ascontiguousarray(words), np.ascontiguousarray(byte.astype(np.uint8).reshape(k // 512, 16, n))


def unpack_weight(words, scales, fmt):
    g, p, n, _ = words.shape
    if fmt == "e4m3":
        vals = np.ascontiguousarray(words).view(ml_dtypes.float8_e4m3fn).astype(np.float64)
    else:
        nib = np.empty((g, p, n, 4), np.uint8)
        nib[..., 0::2] = words & 0xF
        nib[..., 1::2] = words >> 4
        vals = E2M1[nib]
    vals = vals * np.repeat(np.exp2(scales.astype(np.float64) - 127.0), 8, axis=1)[..., None]
    return vals.transpose(0, 1, 3, 2).reshape(g * 512, n)
def pack4(w):
    words, scales = pack_weight(w, "e2m1")
    return words.reshape(words.shape[0], 128, -1), scales


def unpack4(words, scales):
    return unpack_weight(words.reshape(words.shape[0], 128, -1, 2), scales, "e2m1")


D, T, R = 3072, 2048, 512


def setup_inputs():
    s = mx_kscale(T)
    c = mx_kscale(D)
    y = np.random.standard_normal((T, D)) * s[:, None] * c
    v = np.random.standard_normal((T, R)) / np.sqrt(T) / s[:, None]
    left = np.random.standard_normal((D, R)) / np.sqrt(D) / c[:, None]
    y_words, y_scales = pack4(y)
    v_words, v_scales = pack4(v)
    return {"y_words": y_words, "y_scales": y_scales,
            "v_words": v_words, "v_scales": v_scales,
            "sigma": bf(np.random.uniform(0.5, 2.0, R)),
            "vol": bf(1 + 0.1 * np.random.standard_normal(D)),
            "u": bf(left)}


def reference(y_words, y_scales, v_words, v_scales, sigma, vol, u):
    y = unpack4(y_words, y_scales)
    v = unpack4(v_words, v_scales)
    h = y.T @ v
    h = h / f64(sigma)[None, :]
    h = h * f64(vol)[:, None]
    uq = mxq(f64(u), 0, "e4m3")
    hq = mxq(h, 0, "e4m3")
    return uq.T @ hq

@@ -1,0 +1,268 @@
+from contextlib import ExitStack
+
+import concourse.mybir as mybir
+from concourse.masks import make_identity
+
+D, T, R = 3072, 2048, 512
+FLOPS = 2 * T * D * R + 2 * D * R * R
+
+F32 = mybir.dt.float32
+BF16 = mybir.dt.bfloat16
+I32 = mybir.dt.int32
+U32 = mybir.dt.uint32
+U8 = mybir.dt.uint8
+FP8X4 = mybir.dt.float8_e4m3fn_x4
+FP4X4 = mybir.dt.float4_e2m1fn_x4
+MULT = mybir.AluOpType.mult
+
+P = 128
+PACK = 4
+K_PASS = P * PACK
+TIME_PASSES = T // K_PASS
+GROUPS = D // K_PASS
+M_TILES = R // P
+SCALE_RUNS = ((0, 1), (1, 2), (2, 4), (4, 6))
+FIRST_PASSES = (slice(0, 1), slice(1, TIME_PASSES))
+NEAR = 4
+VECTOR_COLUMNS = 320
+DELAY = 2
+ROTATING = 6
+WOVEN = 2
+
+
+def tile_weighted_dmd_operator_s4_kernel(tc, y_words, y_scales, v_words, v_scales, sigma, vol, u, out):
+    nc = tc.nc
+    y_words_i = y_words.bitcast(I32)
+    y_scales_i = y_scales.bitcast(I32)
+    v_words_i = v_words.bitcast(I32)
+    v_scales_i = v_scales.bitcast(I32)
+
+    with ExitStack() as ctx:
+        keep = ctx.enter_context(tc.tile_pool(name="keep", bufs=1))
+        psum = ctx.enter_context(tc.psum_pool(name="psum", bufs=1))
+        ctx.enter_context(tc.manual_schedule())
+
+        def sbuf(name, shape, dtype):
+            return keep.tile(shape, dtype, name=name, align_bytes=64)
+
+        def bank(index, shape):
+            return psum.tile(shape, F32, name="bank%d" % index)
+
+        v_codes = sbuf("v_codes", [P, TIME_PASSES, 2 * R], U8)
+        v_plane = sbuf("v_plane", [P, TIME_PASSES, R], U8)
+        y_raw = [sbuf("y_raw%d" % g, [P, TIME_PASSES, K_PASS // 2], I32) for g in range(GROUPS)]
+        ys_raw = [
+            sbuf("ys_raw%d" % first, [P, TIME_PASSES, (last - first) * K_PASS // 4], I32) for first, last in SCALE_RUNS
+        ]
+        y_codes = [sbuf("y_codes%d" % g, [P, TIME_PASSES, PACK, 2 * P], U8) for g in range(GROUPS)]
+        y_plane = [sbuf("y_plane%d" % g, [P, TIME_PASSES, PACK, P], U8) for g in range(GROUPS)]
+        u_raw = [sbuf("u_raw%d" % g, [P, PACK, R], BF16) for g in range(GROUPS)]
+        u_mixed = [sbuf("u_mixed%d" % g, [P, R, PACK], BF16) for g in range(GROUPS)]
+        u_codes = [sbuf("u_codes%d" % g, [P, R], U32) for g in range(GROUPS)]
+        u_plane = [sbuf("u_plane%d" % g, [P, R], U8) for g in range(GROUPS)]
+        h_rows = [sbuf("h_rows%d" % g, [P, PACK, R], BF16) for g in range(GROUPS)]
+        h_mixed = [sbuf("h_mixed%d" % g, [P, R, PACK], BF16) for g in range(GROUPS)]
+        h_codes = [sbuf("h_codes%d" % g, [P, R], U32) for g in range(GROUPS)]
+        h_plane = [sbuf("h_plane%d" % g, [P, R], U8) for g in range(GROUPS)]
+        ident = sbuf("ident", [P, P], F32)
+        sigma_sb = sbuf("sigma_sb", [P, M_TILES], BF16)
+        sigma_inv = sbuf("sigma_inv", [P, M_TILES], F32)
+        sigma_row = sbuf("sigma_row", [P, R], F32)
+        vol_sb = sbuf("vol_sb", [GROUPS, K_PASS], BF16)
+        vol_rows = sbuf("vol_rows", [P, PACK, P], F32)
+        vol_col = sbuf("vol_col", [P, PACK, GROUPS], F32)
+
+        def load_scale_rows(plane_i, scales_i):
+            for r in range(4):
+                nc.sync.dma_start(out=plane_i[r:P:32, :, :], in_=scales_i[:, r:16:4, :].rearrange("k q w -> q k w"))
+
+        def load_y_scales(run):
+            first, last = SCALE_RUNS[run]
+            load_scale_rows(ys_raw[run], y_scales_i[:, :, first * P : last * P])
+
+        def load_y(g, passes):
+            nc.sync.dma_start(
+                out=y_raw[g][:, passes, :], in_=y_words_i[passes, :, 256 * g : 256 * (g + 1)].rearrange("k p w -> p k w")
+            )
+
+        def load_v(passes):
+            nc.sync.dma_start(out=v_codes[:, passes, :].bitcast(I32), in_=v_words_i[passes].rearrange("k p w -> p k w"))
+
+        def load_u(g):
+            rows = u[K_PASS * g : K_PASS * (g + 1), :].rearrange("(a t r) c -> r a t c", t=PACK, r=4)
+            for r in range(4):
+                nc.sync.dma_start(out=u_raw[g][r:P:4, :, :], in_=rows[r])
+
+        def sort_y_scales(g):
+            run = [i for i, (first, last) in enumerate(SCALE_RUNS) if first <= g < last][0]
+            at = (g - SCALE_RUNS[run][0]) * P
+            nc.vector.tensor_copy(
+                out=y_plane[g][:].bitcast(I32).rearrange("p k t (b i) -> p k b t i", i=4),
+                in_=ys_raw[run][:, :, at : at + P].rearrange("p k (b i t) -> p k b t i", i=4, t=PACK),
+            )
+
+        def sort_y_codes(g, passes):
+            nc.vector.tensor_copy(
+                out=y_codes[g][:, passes, :, :].bitcast(I32).rearrange("p k t (a w) -> p k t a w", w=2),
+                in_=y_raw[g][:, passes, :].rearrange("p k (a t w) -> p k t a w", t=PACK, w=2),
+            )
+
+        def sort_y(g):
+            sort_y_scales(g)
+            sort_y_codes(g, every_pass)
+
+        def interleave(copy, mixed, rows, first, last):
+            copy(
+                out=mixed[:, first:last, :].rearrange("p (c i) t -> p c t i", i=NEAR),
+                in_=rows[:, :, first:last].rearrange("p t (c i) -> p c t i", i=NEAR),
+            )
+
+        def quantize(codes, plane, mixed):
+            nc.vector.quantize_mx(
+                out=codes[:].bitcast(FP8X4), scales=plane[:], in_=mixed[:].rearrange("p c t -> p (c t)")
+            )
+
+        def stage_1_pass(acc, g, t, k):
+            nc.tensor.matmul_mx(
+                out=acc[:],
+                lhsT=y_codes[g][:, k, t, :].bitcast(FP4X4),
+                lhsT_scale=y_plane[g][:, k, t, :],
+                rhs=v_codes[:, k, :].bitcast(FP4X4),
+                rhs_scale=v_plane[:, k, :],
+                start=(k == 0),
+                stop=(k == TIME_PASSES - 1),
+            )
+
+        def weigh(acc, g, t):
+            nc.vector.scalar_tensor_tensor(
+                out=h_rows[g][:, t, :], in0=acc[:], scalar=vol_col[:, t, g : g + 1], in1=sigma_row[:], op0=MULT, op1=MULT
+            )
+
+        def stage_1(g, t):
+            acc = bank((PACK * g + t) % ROTATING, [P, R])
+            for k in range(TIME_PASSES):
+                stage_1_pass(acc, g, t, k)
+            weigh(acc, g, t)
+
+        def stage_2(acc, g, m, cols):
+            rows = slice(P * m, P * (m + 1))
+            nc.tensor.matmul_mx(
+                out=acc[:],
+                lhsT=u_codes[g][:, rows].bitcast(FP8X4),
+                lhsT_scale=u_plane[g][:, rows],
+                rhs=h_codes[g][:, cols].bitcast(FP8X4),
+                rhs_scale=h_plane[g][:, cols],
+                start=(g == 0),
+                stop=(g == GROUPS - 1),
+            )
+
+        def store(copy, acc, m, cols):
+            result = sbuf("result%d_%d" % (m, cols.start), [P, cols.stop - cols.start], F32)
+            copy(out=result[:], in_=acc[:])
+            nc.sync.dma_start(out=out[P * m : P * (m + 1), cols], in_=result[:])
+
+        every_pass = slice(0, TIME_PASSES)
+        whole = slice(0, R)
+        last = GROUPS - 1
+        nc.gpsimd.dma_start(out=sigma_sb[:], in_=sigma.rearrange("(p m) -> p m", m=M_TILES))
+        nc.gpsimd.dma_start(out=vol_sb[:], in_=vol.rearrange("(g c) -> g c", c=K_PASS))
+        make_identity(nc, ident[:])
+        v_plane_i = v_plane[:].bitcast(I32)
+        nc.vector.memset(ys_raw[0][:], 0)
+        nc.vector.memset(v_plane_i, 0)
+        nc.vector.memset(vol_rows[:], 0.0)
+        for run in range(1, len(SCALE_RUNS)):
+            nc.vector.memset(ys_raw[run][:], 0)
+
+        load_y(0, FIRST_PASSES[0])
+        load_v(FIRST_PASSES[0])
+        load_y_scales(0)
+        load_scale_rows(v_plane_i, v_scales_i)
+        load_y(0, FIRST_PASSES[1])
+        load_v(FIRST_PASSES[1])
+        load_u(0)
+        load_y_scales(1)
+        load_y(1, every_pass)
+        load_u(1)
+        load_y_scales(2)
+        load_y(2, every_pass)
+        load_u(2)
+        load_y(3, every_pass)
+        load_y_scales(3)
+        load_u(3)
+        for g in range(4, GROUPS):
+            load_y(g, every_pass)
+            load_u(g)
+
+        sort_y_codes(0, FIRST_PASSES[0])
+        sort_y_scales(0)
+        first_acc = [bank(t, [P, R]) for t in range(PACK)]
+        for t in range(PACK):
+            stage_1_pass(first_acc[t], 0, t, 0)
+
+        nc.vector.reciprocal(out=sigma_inv[:], in_=sigma_sb[:])
+        nc.scalar.copy(
+            out=vol_rows[0:GROUPS, :, :].rearrange("g t (a r) -> g t a r", r=4),
+            in_=vol_sb[:].rearrange("g (a t r) -> g t a r", t=PACK, r=4),
+        )
+        sigma_ps = bank(ROTATING, [P, M_TILES, P])
+        for m in range(M_TILES):
+            nc.tensor.transpose(sigma_ps[:, m, :], sigma_inv[:, m : m + 1].to_broadcast([P, P]), ident[:])
+        vol_ps = bank(ROTATING + 1, [P, PACK, P])
+        for t in range(PACK):
+            nc.tensor.transpose(vol_ps[:, t, :], vol_rows[:, t, :], ident[:])
+        nc.scalar.copy(out=sigma_row[:].rearrange("p (n m) -> p n m", m=M_TILES), in_=sigma_ps[:].rearrange("p m n -> p n m"))
+        nc.scalar.copy(out=vol_col[:], in_=vol_ps[:, :, 0:GROUPS])
+        out_acc = [bank(ROTATING + m, [P, R]) for m in range(WOVEN)]
+
+        sort_y_codes(0, slice(1, 2))
+        sort_y_codes(0, slice(2, TIME_PASSES))
+        for k in range(1, TIME_PASSES):
+            for t in range(PACK):
+                stage_1_pass(first_acc[t], 0, t, k)
+        interleave(nc.scalar.copy, u_mixed[0], u_raw[0], 0, R)
+        interleave(nc.scalar.copy, u_mixed[1], u_raw[1], 0, R)
+        sort_y(1)
+        quantize(u_codes[0], u_plane[0], u_mixed[0])
+        for t in range(PACK):
+            weigh(first_acc[t], 0, t)
+
+        for g in range(1, GROUPS):
+            interleave(nc.scalar.copy, h_mixed[g - 1], h_rows[g - 1], 0, R)
+            if g < last:
+                interleave(nc.scalar.copy, u_mixed[g + 1], u_raw[g + 1], 0, R)
+            stage_1(g, 0)
+            if g >= DELAY:
+                quantize(h_codes[g - DELAY], h_plane[g - DELAY], h_mixed[g - DELAY])
+            stage_1(g, 1)
+            if g < last:
+                sort_y(g + 1)
+                stage_1(g, 2)
+                quantize(u_codes[g], u_plane[g], u_mixed[g])
+            else:
+                quantize(u_codes[g], u_plane[g], u_mixed[g])
+                stage_1(g, 2)
+                quantize(h_codes[g - 1], h_plane[g - 1], h_mixed[g - 1])
+            stage_1(g, 3)
+            if DELAY <= g < last:
+                for m in range(WOVEN):
+                    stage_2(out_acc[m], g - DELAY, m, whole)
+
+        interleave(nc.vector.tensor_copy, h_mixed[last], h_rows[last], 0, VECTOR_COLUMNS)
+        interleave(nc.scalar.copy, h_mixed[last], h_rows[last], VECTOR_COLUMNS, R)
+        quantize(h_codes[last], h_plane[last], h_mixed[last])
+        for g in range(last - DELAY, last):
+            for m in range(WOVEN):
+                stage_2(out_acc[m], g, m, whole)
+        out_acc.append(bank(0, [P, R]))
+        for g in range(last):
+            stage_2(out_acc[WOVEN], g, WOVEN, whole)
+        for m in range(WOVEN + 1):
+            stage_2(out_acc[m], last, m, whole)
+            store(nc.scalar.copy if m % 2 == 0 else nc.vector.tensor_copy, out_acc[m], m, whole)
+        for half in range(2):
+            cols = slice(half * R // 2, (half + 1) * R // 2)
+            acc = bank(1 + half, [P, R // 2])
+            for g in range(GROUPS):
+                stage_2(acc, g, M_TILES - 1, cols)
+            store(nc.vector.tensor_copy if half == 0 else nc.scalar.copy, acc, M_TILES - 1, cols)

@@ -24,10 +24,10 @@ M_TILES = R // P
 SCALE_RUNS = ((0, 1), (1, 2), (2, 4), (4, 6))
 FIRST_PASSES = (slice(0, 1), slice(1, TIME_PASSES))
 NEAR = 4
-VECTOR_COLUMNS = 320
+VECTOR_COLUMNS = 256
 DELAY = 2
-ROTATING = 6
-WOVEN = 2
+ROTATING = 5
+WOVEN = 3
 
 
 def tile_weighted_dmd_operator_s4_kernel(tc, y_words, y_scales, v_words, v_scales, sigma, vol, u, out):
@@ -139,8 +139,8 @@ def tile_weighted_dmd_operator_s4_kernel(tc, y_words, y_scales, v_words, v_scale
             )
 
         def stage_1(g, t):
-            acc = bank((PACK * g + t) % ROTATING, [P, R])
-            for k in range(TIME_PASSES):
+            acc = first_acc[t] if g == 0 else bank((PACK * g + t) % ROTATING, [P, R])
+            for k in range(1 if g == 0 else 0, TIME_PASSES):
                 stage_1_pass(acc, g, t, k)
             weigh(acc, g, t)
 
@@ -164,8 +164,10 @@ def tile_weighted_dmd_operator_s4_kernel(tc, y_words, y_scales, v_words, v_scale
         every_pass = slice(0, TIME_PASSES)
         whole = slice(0, R)
         last = GROUPS - 1
-        nc.gpsimd.dma_start(out=sigma_sb[:], in_=sigma.rearrange("(p m) -> p m", m=M_TILES))
-        nc.gpsimd.dma_start(out=vol_sb[:], in_=vol.rearrange("(g c) -> g c", c=K_PASS))
+        nc.scalar.dma_start(out=sigma_sb[:], in_=sigma.rearrange("(p m) -> p m", m=M_TILES))
+        vol_by_group = vol.rearrange("(g c) -> g c", c=K_PASS)
+        for rows in (slice(0, 4), slice(4, GROUPS)):
+            nc.scalar.dma_start(out=vol_sb[rows, :], in_=vol_by_group[rows, :])
         make_identity(nc, ident[:])
         v_plane_i = v_plane[:].bitcast(I32)
         nc.vector.memset(ys_raw[0][:], 0)
@@ -194,14 +196,8 @@ def tile_weighted_dmd_operator_s4_kernel(tc, y_words, y_scales, v_words, v_scale
             load_y(g, every_pass)
             load_u(g)
 
-        sort_y_codes(0, FIRST_PASSES[0])
-        sort_y_scales(0)
-        first_acc = [bank(t, [P, R]) for t in range(PACK)]
-        for t in range(PACK):
-            stage_1_pass(first_acc[t], 0, t, 0)
-
         nc.vector.reciprocal(out=sigma_inv[:], in_=sigma_sb[:])
-        nc.scalar.copy(
+        nc.vector.tensor_copy(
             out=vol_rows[0:GROUPS, :, :].rearrange("g t (a r) -> g t a r", r=4),
             in_=vol_sb[:].rearrange("g (a t r) -> g t a r", t=PACK, r=4),
         )
@@ -215,20 +211,18 @@ def tile_weighted_dmd_operator_s4_kernel(tc, y_words, y_scales, v_words, v_scale
         nc.scalar.copy(out=vol_col[:], in_=vol_ps[:, :, 0:GROUPS])
         out_acc = [bank(ROTATING + m, [P, R]) for m in range(WOVEN)]
 
+        sort_y_codes(0, FIRST_PASSES[0])
+        sort_y_scales(0)
+        first_acc = [bank(t, [P, R]) for t in range(PACK)]
+        for t in range(PACK):
+            stage_1_pass(first_acc[t], 0, t, 0)
         sort_y_codes(0, slice(1, 2))
         sort_y_codes(0, slice(2, TIME_PASSES))
-        for k in range(1, TIME_PASSES):
-            for t in range(PACK):
-                stage_1_pass(first_acc[t], 0, t, k)
         interleave(nc.scalar.copy, u_mixed[0], u_raw[0], 0, R)
-        interleave(nc.scalar.copy, u_mixed[1], u_raw[1], 0, R)
-        sort_y(1)
-        quantize(u_codes[0], u_plane[0], u_mixed[0])
-        for t in range(PACK):
-            weigh(first_acc[t], 0, t)
 
-        for g in range(1, GROUPS):
-            interleave(nc.scalar.copy, h_mixed[g - 1], h_rows[g - 1], 0, R)
+        for g in range(GROUPS):
+            if g > 0:
+                interleave(nc.scalar.copy, h_mixed[g - 1], h_rows[g - 1], 0, R)
             if g < last:
                 interleave(nc.scalar.copy, u_mixed[g + 1], u_raw[g + 1], 0, R)
             stage_1(g, 0)
@@ -242,7 +236,6 @@ def tile_weighted_dmd_operator_s4_kernel(tc, y_words, y_scales, v_words, v_scale
             else:
                 quantize(u_codes[g], u_plane[g], u_mixed[g])
                 stage_1(g, 2)
-                quantize(h_codes[g - 1], h_plane[g - 1], h_mixed[g - 1])
             stage_1(g, 3)
             if DELAY <= g < last:
                 for m in range(WOVEN):
@@ -250,19 +243,22 @@ def tile_weighted_dmd_operator_s4_kernel(tc, y_words, y_scales, v_words, v_scale
 
         interleave(nc.vector.tensor_copy, h_mixed[last], h_rows[last], 0, VECTOR_COLUMNS)
         interleave(nc.scalar.copy, h_mixed[last], h_rows[last], VECTOR_COLUMNS, R)
+        quantize(h_codes[last - 1], h_plane[last - 1], h_mixed[last - 1])
         quantize(h_codes[last], h_plane[last], h_mixed[last])
-        for g in range(last - DELAY, last):
-            for m in range(WOVEN):
-                stage_2(out_acc[m], g, m, whole)
-        out_acc.append(bank(0, [P, R]))
+        halves = [slice(0, R // 2), slice(R // 2, R)]
+        half_acc = [bank((PACK * GROUPS + half) % ROTATING, [P, R // 2]) for half in range(2)]
+        for m in range(WOVEN):
+            stage_2(out_acc[m], last - DELAY, m, whole)
         for g in range(last):
-            stage_2(out_acc[WOVEN], g, WOVEN, whole)
-        for m in range(WOVEN + 1):
+            for half in range(2):
+                stage_2(half_acc[half], g, WOVEN, halves[half])
+        for m in range(WOVEN):
+            stage_2(out_acc[m], last - 1, m, whole)
+        for m in range(WOVEN):
             stage_2(out_acc[m], last, m, whole)
             store(nc.scalar.copy if m % 2 == 0 else nc.vector.tensor_copy, out_acc[m], m, whole)
         for half in range(2):
-            cols = slice(half * R // 2, (half + 1) * R // 2)
-            acc = bank(1 + half, [P, R // 2])
-            for g in range(GROUPS):
-                stage_2(acc, g, M_TILES - 1, cols)
+            acc = half_acc[half]
+            cols = halves[half]
+            stage_2(acc, last, WOVEN, cols)
             store(nc.vector.tensor_copy if half == 0 else nc.scalar.copy, acc, M_TILES - 1, cols)

@@ -16,18 +16,28 @@ FP4X4 = mybir.dt.float4_e2m1fn_x4
 MULT = mybir.AluOpType.mult
 
 P = 128
-PACK = 4
-K_PASS = P * PACK
+SLOTS = 4
+RUN = 4
+K_PASS = P * SLOTS
 TIME_PASSES = T // K_PASS
 GROUPS = D // K_PASS
-M_TILES = R // P
-SCALE_RUNS = ((0, 1), (1, 2), (2, 4), (4, 6))
-FIRST_PASSES = (slice(0, 1), slice(1, TIME_PASSES))
+LAST = GROUPS - 1
+ROW_TILES = R // P
+CODE_INTS = K_PASS // 2
+SCALE_INTS = K_PASS // 4
+LIVE_ROWS = 4
 NEAR = 4
-VECTOR_COLUMNS = 256
-DELAY = 2
-ROTATING = 5
-WOVEN = 3
+
+SCALE_RANGES = ((0, 1), (1, 2), (2, 4), (4, 6))
+WIDE_TILES = ROW_TILES - 1
+ROTATING = 8 - WIDE_TILES
+LAG = 2
+WOVEN = 2
+U_SHARE = 128
+U_SHARED_FROM = GROUPS - 2
+H_SHARE = 320
+WARM_BEFORE = 16
+WARM_AFTER = 12
 
 
 def tile_weighted_dmd_operator_s4_kernel(tc, y_words, y_scales, v_words, v_scales, sigma, vol, u, out):
@@ -36,6 +46,12 @@ def tile_weighted_dmd_operator_s4_kernel(tc, y_words, y_scales, v_words, v_scale
     y_scales_i = y_scales.bitcast(I32)
     v_words_i = v_words.bitcast(I32)
     v_scales_i = v_scales.bitcast(I32)
+    first_pass = slice(0, 1)
+    later_passes = slice(1, TIME_PASSES)
+    pass_pairs = (slice(0, 2), slice(2, TIME_PASSES))
+    all_passes = slice(0, TIME_PASSES)
+    all_columns = slice(0, R)
+    halves = (slice(0, R // 2), slice(R // 2, R))
 
     with ExitStack() as ctx:
         keep = ctx.enter_context(tc.tile_pool(name="keep", bufs=1))
@@ -45,82 +61,86 @@ def tile_weighted_dmd_operator_s4_kernel(tc, y_words, y_scales, v_words, v_scale
         def sbuf(name, shape, dtype):
             return keep.tile(shape, dtype, name=name, align_bytes=64)
 
+        def per_group(name, shape, dtype):
+            return [sbuf("%s%d" % (name, g), shape, dtype) for g in range(GROUPS)]
+
         def bank(index, shape):
             return psum.tile(shape, F32, name="bank%d" % index)
 
         v_codes = sbuf("v_codes", [P, TIME_PASSES, 2 * R], U8)
         v_plane = sbuf("v_plane", [P, TIME_PASSES, R], U8)
-        y_raw = [sbuf("y_raw%d" % g, [P, TIME_PASSES, K_PASS // 2], I32) for g in range(GROUPS)]
-        ys_raw = [
-            sbuf("ys_raw%d" % first, [P, TIME_PASSES, (last - first) * K_PASS // 4], I32) for first, last in SCALE_RUNS
-        ]
-        y_codes = [sbuf("y_codes%d" % g, [P, TIME_PASSES, PACK, 2 * P], U8) for g in range(GROUPS)]
-        y_plane = [sbuf("y_plane%d" % g, [P, TIME_PASSES, PACK, P], U8) for g in range(GROUPS)]
-        u_raw = [sbuf("u_raw%d" % g, [P, PACK, R], BF16) for g in range(GROUPS)]
-        u_mixed = [sbuf("u_mixed%d" % g, [P, R, PACK], BF16) for g in range(GROUPS)]
-        u_codes = [sbuf("u_codes%d" % g, [P, R], U32) for g in range(GROUPS)]
-        u_plane = [sbuf("u_plane%d" % g, [P, R], U8) for g in range(GROUPS)]
-        h_rows = [sbuf("h_rows%d" % g, [P, PACK, R], BF16) for g in range(GROUPS)]
-        h_mixed = [sbuf("h_mixed%d" % g, [P, R, PACK], BF16) for g in range(GROUPS)]
-        h_codes = [sbuf("h_codes%d" % g, [P, R], U32) for g in range(GROUPS)]
-        h_plane = [sbuf("h_plane%d" % g, [P, R], U8) for g in range(GROUPS)]
+        y_raw = per_group("y_raw", [P, TIME_PASSES, CODE_INTS], I32)
+        y_scale_raw = [sbuf("y_scale_raw%d" % lo, [P, TIME_PASSES, (hi - lo) * SCALE_INTS], I32) for lo, hi in SCALE_RANGES]
+        y_codes = per_group("y_codes", [P, TIME_PASSES, SLOTS, 2 * P], U8)
+        y_plane = per_group("y_plane", [P, TIME_PASSES, SLOTS, P], U8)
+        u_rows = per_group("u_rows", [P, SLOTS, R], BF16)
+        u_mixed = per_group("u_mixed", [P, R, SLOTS], BF16)
+        u_codes = per_group("u_codes", [P, R], U32)
+        u_plane = per_group("u_plane", [P, R], U8)
+        h_rows = per_group("h_rows", [P, SLOTS, R], BF16)
+        h_mixed = per_group("h_mixed", [P, R, SLOTS], BF16)
+        h_codes = per_group("h_codes", [P, R], U32)
+        h_plane = per_group("h_plane", [P, R], U8)
         ident = sbuf("ident", [P, P], F32)
-        sigma_sb = sbuf("sigma_sb", [P, M_TILES], BF16)
-        sigma_inv = sbuf("sigma_inv", [P, M_TILES], F32)
-        sigma_row = sbuf("sigma_row", [P, R], F32)
+        sigma_sb = sbuf("sigma_sb", [P, R // P], BF16)
+        sigma_inv = sbuf("sigma_inv", [P, R // P], F32)
+        sigma_inv_row = sbuf("sigma_inv_row", [P, R], F32)
         vol_sb = sbuf("vol_sb", [GROUPS, K_PASS], BF16)
-        vol_rows = sbuf("vol_rows", [P, PACK, P], F32)
-        vol_col = sbuf("vol_col", [P, PACK, GROUPS], F32)
+        vol_rows = sbuf("vol_rows", [P, SLOTS, P], F32)
+        vol_col = sbuf("vol_col", [P, SLOTS, GROUPS], F32)
 
-        def load_scale_rows(plane_i, scales_i):
-            for r in range(4):
-                nc.sync.dma_start(out=plane_i[r:P:32, :, :], in_=scales_i[:, r:16:4, :].rearrange("k q w -> q k w"))
+        warm_in = sbuf("warm_in", [P, P, SLOTS], BF16)
+        warm_codes = sbuf("warm_codes", [P, P], U32)
+        warm_plane = sbuf("warm_plane", [P, P], U8)
 
-        def load_y_scales(run):
-            first, last = SCALE_RUNS[run]
-            load_scale_rows(ys_raw[run], y_scales_i[:, :, first * P : last * P])
+        def load_scale_rows(plane_i, scales_i, rows):
+            for r in rows:
+                nc.sync.dma_start(out=plane_i[r:P:32, :, :], in_=scales_i[:, r:16:LIVE_ROWS, :].rearrange("k q w -> q k w"))
+
+        def load_y_scales(n, rows):
+            lo, hi = SCALE_RANGES[n]
+            load_scale_rows(y_scale_raw[n], y_scales_i[:, :, lo * SCALE_INTS : hi * SCALE_INTS], rows)
 
         def load_y(g, passes):
-            nc.sync.dma_start(
-                out=y_raw[g][:, passes, :], in_=y_words_i[passes, :, 256 * g : 256 * (g + 1)].rearrange("k p w -> p k w")
-            )
+            source = y_words_i[passes, :, CODE_INTS * g : CODE_INTS * (g + 1)]
+            nc.sync.dma_start(out=y_raw[g][:, passes, :], in_=source.rearrange("k p w -> p k w"))
 
         def load_v(passes):
             nc.sync.dma_start(out=v_codes[:, passes, :].bitcast(I32), in_=v_words_i[passes].rearrange("k p w -> p k w"))
 
         def load_u(g):
-            rows = u[K_PASS * g : K_PASS * (g + 1), :].rearrange("(a t r) c -> r a t c", t=PACK, r=4)
-            for r in range(4):
-                nc.sync.dma_start(out=u_raw[g][r:P:4, :, :], in_=rows[r])
+            rows = u[K_PASS * g : K_PASS * (g + 1), :].rearrange("(a t r) c -> r a t c", t=SLOTS, r=RUN)
+            for r in range(RUN):
+                nc.sync.dma_start(out=u_rows[g][r:P:RUN, :, :], in_=rows[r])
 
         def sort_y_scales(g):
-            run = [i for i, (first, last) in enumerate(SCALE_RUNS) if first <= g < last][0]
-            at = (g - SCALE_RUNS[run][0]) * P
+            n = [i for i, (lo, hi) in enumerate(SCALE_RANGES) if lo <= g < hi][0]
+            at = (g - SCALE_RANGES[n][0]) * SCALE_INTS
             nc.vector.tensor_copy(
-                out=y_plane[g][:].bitcast(I32).rearrange("p k t (b i) -> p k b t i", i=4),
-                in_=ys_raw[run][:, :, at : at + P].rearrange("p k (b i t) -> p k b t i", i=4, t=PACK),
+                out=y_plane[g][:].bitcast(I32).rearrange("p k t (b i) -> p k b t i", i=NEAR),
+                in_=y_scale_raw[n][:, :, at : at + SCALE_INTS].rearrange("p k (b i t) -> p k b t i", i=NEAR, t=SLOTS),
             )
 
         def sort_y_codes(g, passes):
             nc.vector.tensor_copy(
                 out=y_codes[g][:, passes, :, :].bitcast(I32).rearrange("p k t (a w) -> p k t a w", w=2),
-                in_=y_raw[g][:, passes, :].rearrange("p k (a t w) -> p k t a w", t=PACK, w=2),
+                in_=y_raw[g][:, passes, :].rearrange("p k (a t w) -> p k t a w", t=SLOTS, w=2),
             )
 
-        def sort_y(g):
-            sort_y_scales(g)
-            sort_y_codes(g, every_pass)
-
-        def interleave(copy, mixed, rows, first, last):
+        def interleave(copy, mixed, rows, lo, hi):
             copy(
-                out=mixed[:, first:last, :].rearrange("p (c i) t -> p c t i", i=NEAR),
-                in_=rows[:, :, first:last].rearrange("p t (c i) -> p c t i", i=NEAR),
+                out=mixed[:, lo:hi, :].rearrange("p (c i) t -> p c t i", i=NEAR),
+                in_=rows[:, :, lo:hi].rearrange("p t (c i) -> p c t i", i=NEAR),
             )
 
         def quantize(codes, plane, mixed):
-            nc.vector.quantize_mx(
-                out=codes[:].bitcast(FP8X4), scales=plane[:], in_=mixed[:].rearrange("p c t -> p (c t)")
-            )
+            nc.vector.quantize_mx(out=codes[:].bitcast(FP8X4), scales=plane[:], in_=mixed[:].rearrange("p c t -> p (c t)"))
+
+        def quantize_u(g):
+            quantize(u_codes[g], u_plane[g], u_mixed[g])
+
+        def quantize_h(g):
+            quantize(h_codes[g], h_plane[g], h_mixed[g])
 
         def stage_1_pass(acc, g, t, k):
             nc.tensor.matmul_mx(
@@ -133,132 +153,155 @@ def tile_weighted_dmd_operator_s4_kernel(tc, y_words, y_scales, v_words, v_scale
                 stop=(k == TIME_PASSES - 1),
             )
 
-        def weigh(acc, g, t):
-            nc.vector.scalar_tensor_tensor(
-                out=h_rows[g][:, t, :], in0=acc[:], scalar=vol_col[:, t, g : g + 1], in1=sigma_row[:], op0=MULT, op1=MULT
-            )
-
         def stage_1(g, t):
-            acc = first_acc[t] if g == 0 else bank((PACK * g + t) % ROTATING, [P, R])
+            acc = first_acc[t] if g == 0 else bank((SLOTS * g + t) % ROTATING, [P, R])
             for k in range(1 if g == 0 else 0, TIME_PASSES):
                 stage_1_pass(acc, g, t, k)
-            weigh(acc, g, t)
+            nc.vector.scalar_tensor_tensor(
+                out=h_rows[g][:, t, :], in0=acc[:], scalar=vol_col[:, t, g : g + 1], in1=sigma_inv_row[:], op0=MULT, op1=MULT
+            )
 
-        def stage_2(acc, g, m, cols):
+        def stage_2(acc, g, m, columns):
             rows = slice(P * m, P * (m + 1))
             nc.tensor.matmul_mx(
                 out=acc[:],
                 lhsT=u_codes[g][:, rows].bitcast(FP8X4),
                 lhsT_scale=u_plane[g][:, rows],
-                rhs=h_codes[g][:, cols].bitcast(FP8X4),
-                rhs_scale=h_plane[g][:, cols],
+                rhs=h_codes[g][:, columns].bitcast(FP8X4),
+                rhs_scale=h_plane[g][:, columns],
                 start=(g == 0),
-                stop=(g == GROUPS - 1),
+                stop=(g == LAST),
             )
 
-        def store(copy, acc, m, cols):
-            result = sbuf("result%d_%d" % (m, cols.start), [P, cols.stop - cols.start], F32)
-            copy(out=result[:], in_=acc[:])
-            nc.sync.dma_start(out=out[P * m : P * (m + 1), cols], in_=result[:])
+        def warm_up(count):
+            acc = bank(ROTATING - 1, [P, P])
+            for step in range(count):
+                nc.tensor.matmul_mx(
+                    out=acc[:],
+                    lhsT=warm_codes[:].bitcast(FP8X4),
+                    lhsT_scale=warm_plane[:],
+                    rhs=warm_codes[:].bitcast(FP8X4),
+                    rhs_scale=warm_plane[:],
+                    start=(step == 0),
+                    stop=(step == count - 1),
+                )
 
-        every_pass = slice(0, TIME_PASSES)
-        whole = slice(0, R)
-        last = GROUPS - 1
-        nc.scalar.dma_start(out=sigma_sb[:], in_=sigma.rearrange("(p m) -> p m", m=M_TILES))
-        vol_by_group = vol.rearrange("(g c) -> g c", c=K_PASS)
-        for rows in (slice(0, 4), slice(4, GROUPS)):
-            nc.scalar.dma_start(out=vol_sb[rows, :], in_=vol_by_group[rows, :])
+        def store(copy, acc, m, columns):
+            result = sbuf("result%d_%d" % (m, columns.start), [P, columns.stop - columns.start], F32)
+            copy(out=result[:], in_=acc[:])
+            nc.sync.dma_start(out=out[P * m : P * (m + 1), columns], in_=result[:])
+
+        nc.gpsimd.memset(warm_in[:], 1.0)
         make_identity(nc, ident[:])
         v_plane_i = v_plane[:].bitcast(I32)
-        nc.vector.memset(ys_raw[0][:], 0)
+        nc.vector.memset(y_scale_raw[0][:], 0)
+        quantize(warm_codes, warm_plane, warm_in)
+        warm_up(WARM_BEFORE)
         nc.vector.memset(v_plane_i, 0)
         nc.vector.memset(vol_rows[:], 0.0)
-        for run in range(1, len(SCALE_RUNS)):
-            nc.vector.memset(ys_raw[run][:], 0)
+        nc.vector.memset(y_scale_raw[1][:], 0)
 
-        load_y(0, FIRST_PASSES[0])
-        load_v(FIRST_PASSES[0])
-        load_y_scales(0)
-        load_scale_rows(v_plane_i, v_scales_i)
-        load_y(0, FIRST_PASSES[1])
-        load_v(FIRST_PASSES[1])
+        nc.sync.dma_start(out=sigma_sb[:], in_=sigma.rearrange("(p m) -> p m", m=R // P))
+        vol_by_group = vol.rearrange("(g c) -> g c", c=K_PASS)
+        for groups in (slice(0, 4), slice(4, GROUPS)):
+            nc.sync.dma_start(out=vol_sb[groups, :], in_=vol_by_group[groups, :])
+        load_y(0, first_pass)
+        load_v(first_pass)
+        load_y_scales(0, range(LIVE_ROWS - 1))
+        load_y(0, later_passes)
+        load_y_scales(0, [LIVE_ROWS - 1])
+        load_scale_rows(v_plane_i, v_scales_i, range(LIVE_ROWS))
+        load_v(later_passes)
         load_u(0)
-        load_y_scales(1)
-        load_y(1, every_pass)
+        load_y_scales(1, range(LIVE_ROWS))
+        for passes in pass_pairs:
+            load_y(1, passes)
         load_u(1)
-        load_y_scales(2)
-        load_y(2, every_pass)
-        load_u(2)
-        load_y(3, every_pass)
-        load_y_scales(3)
-        load_u(3)
-        for g in range(4, GROUPS):
-            load_y(g, every_pass)
-            load_u(g)
 
         nc.vector.reciprocal(out=sigma_inv[:], in_=sigma_sb[:])
         nc.vector.tensor_copy(
-            out=vol_rows[0:GROUPS, :, :].rearrange("g t (a r) -> g t a r", r=4),
-            in_=vol_sb[:].rearrange("g (a t r) -> g t a r", t=PACK, r=4),
+            out=vol_rows[0:GROUPS, :, :].rearrange("g t (a r) -> g t a r", r=RUN),
+            in_=vol_sb[:].rearrange("g (a t r) -> g t a r", t=SLOTS, r=RUN),
         )
-        sigma_ps = bank(ROTATING, [P, M_TILES, P])
-        for m in range(M_TILES):
+        sigma_ps = bank(ROTATING, [P, R // P, P])
+        for m in range(R // P):
             nc.tensor.transpose(sigma_ps[:, m, :], sigma_inv[:, m : m + 1].to_broadcast([P, P]), ident[:])
-        vol_ps = bank(ROTATING + 1, [P, PACK, P])
-        for t in range(PACK):
+        vol_ps = bank(ROTATING + 1, [P, SLOTS, P])
+        for t in range(SLOTS):
             nc.tensor.transpose(vol_ps[:, t, :], vol_rows[:, t, :], ident[:])
-        nc.scalar.copy(out=sigma_row[:].rearrange("p (n m) -> p n m", m=M_TILES), in_=sigma_ps[:].rearrange("p m n -> p n m"))
+        nc.scalar.copy(out=sigma_inv_row[:].rearrange("p (n m) -> p n m", n=P), in_=sigma_ps[:].rearrange("p m n -> p n m"))
         nc.scalar.copy(out=vol_col[:], in_=vol_ps[:, :, 0:GROUPS])
-        out_acc = [bank(ROTATING + m, [P, R]) for m in range(WOVEN)]
+        warm_up(WARM_AFTER)
+        wide_acc = [bank(ROTATING + m, [P, R]) for m in range(WIDE_TILES)]
 
-        sort_y_codes(0, FIRST_PASSES[0])
+        sort_y_codes(0, first_pass)
         sort_y_scales(0)
-        first_acc = [bank(t, [P, R]) for t in range(PACK)]
-        for t in range(PACK):
+        first_acc = [bank(t, [P, R]) for t in range(SLOTS)]
+        for t in range(SLOTS):
             stage_1_pass(first_acc[t], 0, t, 0)
         sort_y_codes(0, slice(1, 2))
-        sort_y_codes(0, slice(2, TIME_PASSES))
-        interleave(nc.scalar.copy, u_mixed[0], u_raw[0], 0, R)
+        sort_y_codes(0, pass_pairs[1])
 
+        for n in range(2, len(SCALE_RANGES)):
+            nc.vector.memset(y_scale_raw[n][:], 0)
+        load_y_scales(2, range(LIVE_ROWS))
+        load_y(2, all_passes)
+        load_u(2)
+        load_y(3, all_passes)
+        load_y_scales(3, range(LIVE_ROWS))
+        load_u(3)
+        for g in range(4, GROUPS):
+            load_y(g, all_passes)
+            load_u(g)
+
+        interleave(nc.scalar.copy, u_mixed[0], u_rows[0], 0, R)
         for g in range(GROUPS):
             if g > 0:
                 interleave(nc.scalar.copy, h_mixed[g - 1], h_rows[g - 1], 0, R)
-            if g < last:
-                interleave(nc.scalar.copy, u_mixed[g + 1], u_raw[g + 1], 0, R)
+            if g < LAST:
+                share = U_SHARE if g + 1 >= U_SHARED_FROM else 0
+                interleave(nc.scalar.copy, u_mixed[g + 1], u_rows[g + 1], share, R)
+                if share:
+                    interleave(nc.vector.tensor_copy, u_mixed[g + 1], u_rows[g + 1], 0, share)
             stage_1(g, 0)
-            if g >= DELAY:
-                quantize(h_codes[g - DELAY], h_plane[g - DELAY], h_mixed[g - DELAY])
+            if g >= LAG:
+                quantize_h(g - LAG)
             stage_1(g, 1)
-            if g < last:
-                sort_y(g + 1)
+            if g == LAST:
+                quantize_u(g)
                 stage_1(g, 2)
-                quantize(u_codes[g], u_plane[g], u_mixed[g])
             else:
-                quantize(u_codes[g], u_plane[g], u_mixed[g])
+                sort_y_scales(g + 1)
+                for passes in pass_pairs if g == 0 else [all_passes]:
+                    sort_y_codes(g + 1, passes)
                 stage_1(g, 2)
+                quantize_u(g)
             stage_1(g, 3)
-            if DELAY <= g < last:
-                for m in range(WOVEN):
-                    stage_2(out_acc[m], g - DELAY, m, whole)
+            if 0 <= g - LAG < WOVEN:
+                for m in range(WIDE_TILES):
+                    stage_2(wide_acc[m], g - LAG, m, all_columns)
 
-        interleave(nc.vector.tensor_copy, h_mixed[last], h_rows[last], 0, VECTOR_COLUMNS)
-        interleave(nc.scalar.copy, h_mixed[last], h_rows[last], VECTOR_COLUMNS, R)
-        quantize(h_codes[last - 1], h_plane[last - 1], h_mixed[last - 1])
-        quantize(h_codes[last], h_plane[last], h_mixed[last])
-        halves = [slice(0, R // 2), slice(R // 2, R)]
-        half_acc = [bank((PACK * GROUPS + half) % ROTATING, [P, R // 2]) for half in range(2)]
-        for m in range(WOVEN):
-            stage_2(out_acc[m], last - DELAY, m, whole)
-        for g in range(last):
-            for half in range(2):
-                stage_2(half_acc[half], g, WOVEN, halves[half])
-        for m in range(WOVEN):
-            stage_2(out_acc[m], last - 1, m, whole)
-        for m in range(WOVEN):
-            stage_2(out_acc[m], last, m, whole)
-            store(nc.scalar.copy if m % 2 == 0 else nc.vector.tensor_copy, out_acc[m], m, whole)
-        for half in range(2):
-            acc = half_acc[half]
-            cols = halves[half]
-            stage_2(acc, last, WOVEN, cols)
-            store(nc.vector.tensor_copy if half == 0 else nc.scalar.copy, acc, M_TILES - 1, cols)
+        quantize_h(LAST - 1)
+        interleave(nc.vector.tensor_copy, h_mixed[LAST], h_rows[LAST], 0, H_SHARE)
+        interleave(nc.scalar.copy, h_mixed[LAST], h_rows[LAST], H_SHARE, R)
+        quantize_h(LAST)
+
+        half_acc = [bank((SLOTS * GROUPS + n) % ROTATING, [P, R // 2]) for n in range(2)]
+        for g in range(WOVEN, LAST - 1):
+            for m in range(WIDE_TILES):
+                stage_2(wide_acc[m], g, m, all_columns)
+        for g in range(LAST):
+            for n in range(2):
+                stage_2(half_acc[n], g, WIDE_TILES, halves[n])
+        for m in range(WIDE_TILES - 1):
+            stage_2(wide_acc[m], LAST - 1, m, all_columns)
+
+        copies = (nc.scalar.copy, nc.vector.tensor_copy)
+        for n in range(2):
+            stage_2(half_acc[n], LAST, WIDE_TILES, halves[n])
+            store(copies[n], half_acc[n], WIDE_TILES, halves[n])
+        for m in range(WIDE_TILES):
+            if m == WIDE_TILES - 1:
+                stage_2(wide_acc[m], LAST - 1, m, all_columns)
+            stage_2(wide_acc[m], LAST, m, all_columns)
+            store(copies[m % 2], wide_acc[m], m, all_columns)

@@ -32,12 +32,8 @@ SCALE_RANGES = ((0, 1), (1, 2), (2, 4), (4, 6))
 WIDE_TILES = ROW_TILES - 1
 ROTATING = 8 - WIDE_TILES
 LAG = 2
-WOVEN = 2
-U_SHARE = 128
-U_SHARED_FROM = GROUPS - 2
-H_SHARE = 320
-WARM_BEFORE = 16
-WARM_AFTER = 12
+WOVEN = 3
+H_SHARE = 288
 
 
 def tile_weighted_dmd_operator_s4_kernel(tc, y_words, y_scales, v_words, v_scales, sigma, vol, u, out):
@@ -89,17 +85,13 @@ def tile_weighted_dmd_operator_s4_kernel(tc, y_words, y_scales, v_words, v_scale
         vol_rows = sbuf("vol_rows", [P, SLOTS, P], F32)
         vol_col = sbuf("vol_col", [P, SLOTS, GROUPS], F32)
 
-        warm_in = sbuf("warm_in", [P, P, SLOTS], BF16)
-        warm_codes = sbuf("warm_codes", [P, P], U32)
-        warm_plane = sbuf("warm_plane", [P, P], U8)
-
-        def load_scale_rows(plane_i, scales_i, rows):
-            for r in rows:
+        def load_scale_rows(plane_i, scales_i):
+            for r in range(LIVE_ROWS):
                 nc.sync.dma_start(out=plane_i[r:P:32, :, :], in_=scales_i[:, r:16:LIVE_ROWS, :].rearrange("k q w -> q k w"))
 
-        def load_y_scales(n, rows):
+        def load_y_scales(n):
             lo, hi = SCALE_RANGES[n]
-            load_scale_rows(y_scale_raw[n], y_scales_i[:, :, lo * SCALE_INTS : hi * SCALE_INTS], rows)
+            load_scale_rows(y_scale_raw[n], y_scales_i[:, :, lo * SCALE_INTS : hi * SCALE_INTS])
 
         def load_y(g, passes):
             source = y_words_i[passes, :, CODE_INTS * g : CODE_INTS * (g + 1)]
@@ -173,47 +165,30 @@ def tile_weighted_dmd_operator_s4_kernel(tc, y_words, y_scales, v_words, v_scale
                 stop=(g == LAST),
             )
 
-        def warm_up(count):
-            acc = bank(ROTATING - 1, [P, P])
-            for step in range(count):
-                nc.tensor.matmul_mx(
-                    out=acc[:],
-                    lhsT=warm_codes[:].bitcast(FP8X4),
-                    lhsT_scale=warm_plane[:],
-                    rhs=warm_codes[:].bitcast(FP8X4),
-                    rhs_scale=warm_plane[:],
-                    start=(step == 0),
-                    stop=(step == count - 1),
-                )
-
         def store(copy, acc, m, columns):
             result = sbuf("result%d_%d" % (m, columns.start), [P, columns.stop - columns.start], F32)
             copy(out=result[:], in_=acc[:])
             nc.sync.dma_start(out=out[P * m : P * (m + 1), columns], in_=result[:])
 
-        nc.gpsimd.memset(warm_in[:], 1.0)
         make_identity(nc, ident[:])
         v_plane_i = v_plane[:].bitcast(I32)
         nc.vector.memset(y_scale_raw[0][:], 0)
-        quantize(warm_codes, warm_plane, warm_in)
-        warm_up(WARM_BEFORE)
         nc.vector.memset(v_plane_i, 0)
         nc.vector.memset(vol_rows[:], 0.0)
         nc.vector.memset(y_scale_raw[1][:], 0)
 
-        nc.sync.dma_start(out=sigma_sb[:], in_=sigma.rearrange("(p m) -> p m", m=R // P))
+        nc.scalar.dma_start(out=sigma_sb[:], in_=sigma.rearrange("(p m) -> p m", m=R // P))
         vol_by_group = vol.rearrange("(g c) -> g c", c=K_PASS)
         for groups in (slice(0, 4), slice(4, GROUPS)):
-            nc.sync.dma_start(out=vol_sb[groups, :], in_=vol_by_group[groups, :])
+            nc.scalar.dma_start(out=vol_sb[groups, :], in_=vol_by_group[groups, :])
         load_y(0, first_pass)
         load_v(first_pass)
-        load_y_scales(0, range(LIVE_ROWS - 1))
+        load_y_scales(0)
+        load_scale_rows(v_plane_i, v_scales_i)
         load_y(0, later_passes)
-        load_y_scales(0, [LIVE_ROWS - 1])
-        load_scale_rows(v_plane_i, v_scales_i, range(LIVE_ROWS))
         load_v(later_passes)
         load_u(0)
-        load_y_scales(1, range(LIVE_ROWS))
+        load_y_scales(1)
         for passes in pass_pairs:
             load_y(1, passes)
         load_u(1)
@@ -231,7 +206,6 @@ def tile_weighted_dmd_operator_s4_kernel(tc, y_words, y_scales, v_words, v_scale
             nc.tensor.transpose(vol_ps[:, t, :], vol_rows[:, t, :], ident[:])
         nc.scalar.copy(out=sigma_inv_row[:].rearrange("p (n m) -> p n m", n=P), in_=sigma_ps[:].rearrange("p m n -> p n m"))
         nc.scalar.copy(out=vol_col[:], in_=vol_ps[:, :, 0:GROUPS])
-        warm_up(WARM_AFTER)
         wide_acc = [bank(ROTATING + m, [P, R]) for m in range(WIDE_TILES)]
 
         sort_y_codes(0, first_pass)
@@ -244,11 +218,11 @@ def tile_weighted_dmd_operator_s4_kernel(tc, y_words, y_scales, v_words, v_scale
 
         for n in range(2, len(SCALE_RANGES)):
             nc.vector.memset(y_scale_raw[n][:], 0)
-        load_y_scales(2, range(LIVE_ROWS))
+        load_y_scales(2)
         load_y(2, all_passes)
         load_u(2)
         load_y(3, all_passes)
-        load_y_scales(3, range(LIVE_ROWS))
+        load_y_scales(3)
         load_u(3)
         for g in range(4, GROUPS):
             load_y(g, all_passes)
@@ -259,10 +233,7 @@ def tile_weighted_dmd_operator_s4_kernel(tc, y_words, y_scales, v_words, v_scale
             if g > 0:
                 interleave(nc.scalar.copy, h_mixed[g - 1], h_rows[g - 1], 0, R)
             if g < LAST:
-                share = U_SHARE if g + 1 >= U_SHARED_FROM else 0
-                interleave(nc.scalar.copy, u_mixed[g + 1], u_rows[g + 1], share, R)
-                if share:
-                    interleave(nc.vector.tensor_copy, u_mixed[g + 1], u_rows[g + 1], 0, share)
+                interleave(nc.scalar.copy, u_mixed[g + 1], u_rows[g + 1], 0, R)
             stage_1(g, 0)
             if g >= LAG:
                 quantize_h(g - LAG)
@@ -293,7 +264,7 @@ def tile_weighted_dmd_operator_s4_kernel(tc, y_words, y_scales, v_words, v_scale
         for g in range(LAST):
             for n in range(2):
                 stage_2(half_acc[n], g, WIDE_TILES, halves[n])
-        for m in range(WIDE_TILES - 1):
+        for m in range(WIDE_TILES):
             stage_2(wide_acc[m], LAST - 1, m, all_columns)
 
         copies = (nc.scalar.copy, nc.vector.tensor_copy)
@@ -301,7 +272,5 @@ def tile_weighted_dmd_operator_s4_kernel(tc, y_words, y_scales, v_words, v_scale
             stage_2(half_acc[n], LAST, WIDE_TILES, halves[n])
             store(copies[n], half_acc[n], WIDE_TILES, halves[n])
         for m in range(WIDE_TILES):
-            if m == WIDE_TILES - 1:
-                stage_2(wide_acc[m], LAST - 1, m, all_columns)
             stage_2(wide_acc[m], LAST, m, all_columns)
             store(copies[m % 2], wide_acc[m], m, all_columns)

from contextlib import ExitStack

import concourse.mybir as mybir
from concourse.masks import make_identity

D, T, R = 3072, 2048, 512
FLOPS = 2 * T * D * R + 2 * D * R * R

F32 = mybir.dt.float32
BF16 = mybir.dt.bfloat16
I32 = mybir.dt.int32
U32 = mybir.dt.uint32
U8 = mybir.dt.uint8
FP8X4 = mybir.dt.float8_e4m3fn_x4
FP4X4 = mybir.dt.float4_e2m1fn_x4
MULT = mybir.AluOpType.mult

P = 128
SLOTS = 4
RUN = 4
K_PASS = P * SLOTS
TIME_PASSES = T // K_PASS
GROUPS = D // K_PASS
LAST = GROUPS - 1
ROW_TILES = R // P
CODE_INTS = K_PASS // 2
SCALE_INTS = K_PASS // 4
LIVE_ROWS = 4
NEAR = 4

SCALE_RANGES = ((0, 1), (1, 2), (2, 4), (4, 6))
WIDE_TILES = ROW_TILES - 1
ROTATING = 8 - WIDE_TILES
LAG = 2
WOVEN = 3
H_SHARE = 288


def tile_weighted_dmd_operator_s4_kernel(tc, y_words, y_scales, v_words, v_scales, sigma, vol, u, out):
    nc = tc.nc
    y_words_i = y_words.bitcast(I32)
    y_scales_i = y_scales.bitcast(I32)
    v_words_i = v_words.bitcast(I32)
    v_scales_i = v_scales.bitcast(I32)
    first_pass = slice(0, 1)
    later_passes = slice(1, TIME_PASSES)
    pass_pairs = (slice(0, 2), slice(2, TIME_PASSES))
    all_passes = slice(0, TIME_PASSES)
    all_columns = slice(0, R)
    halves = (slice(0, R // 2), slice(R // 2, R))

    with ExitStack() as ctx:
        keep = ctx.enter_context(tc.tile_pool(name="keep", bufs=1))
        psum = ctx.enter_context(tc.psum_pool(name="psum", bufs=1))
        ctx.enter_context(tc.manual_schedule())

        def sbuf(name, shape, dtype):
            return keep.tile(shape, dtype, name=name, align_bytes=64)

        def per_group(name, shape, dtype):
            return [sbuf("%s%d" % (name, g), shape, dtype) for g in range(GROUPS)]

        def bank(index, shape):
            return psum.tile(shape, F32, name="bank%d" % index)

        v_codes = sbuf("v_codes", [P, TIME_PASSES, 2 * R], U8)
        v_plane = sbuf("v_plane", [P, TIME_PASSES, R], U8)
        y_raw = per_group("y_raw", [P, TIME_PASSES, CODE_INTS], I32)
        y_scale_raw = [sbuf("y_scale_raw%d" % lo, [P, TIME_PASSES, (hi - lo) * SCALE_INTS], I32) for lo, hi in SCALE_RANGES]
        y_codes = per_group("y_codes", [P, TIME_PASSES, SLOTS, 2 * P], U8)
        y_plane = per_group("y_plane", [P, TIME_PASSES, SLOTS, P], U8)
        u_rows = per_group("u_rows", [P, SLOTS, R], BF16)
        u_mixed = per_group("u_mixed", [P, R, SLOTS], BF16)
        u_codes = per_group("u_codes", [P, R], U32)
        u_plane = per_group("u_plane", [P, R], U8)
        h_rows = per_group("h_rows", [P, SLOTS, R], BF16)
        h_mixed = per_group("h_mixed", [P, R, SLOTS], BF16)
        h_codes = per_group("h_codes", [P, R], U32)
        h_plane = per_group("h_plane", [P, R], U8)
        ident = sbuf("ident", [P, P], F32)
        sigma_sb = sbuf("sigma_sb", [P, R // P], BF16)
        sigma_inv = sbuf("sigma_inv", [P, R // P], F32)
        sigma_inv_row = sbuf("sigma_inv_row", [P, R], F32)
        vol_sb = sbuf("vol_sb", [GROUPS, K_PASS], BF16)
        vol_rows = sbuf("vol_rows", [P, SLOTS, P], F32)
        vol_col = sbuf("vol_col", [P, SLOTS, GROUPS], F32)

        def load_scale_rows(plane_i, scales_i):
            for r in range(LIVE_ROWS):
                nc.sync.dma_start(out=plane_i[r:P:32, :, :], in_=scales_i[:, r:16:LIVE_ROWS, :].rearrange("k q w -> q k w"))

        def load_y_scales(n):
            lo, hi = SCALE_RANGES[n]
            load_scale_rows(y_scale_raw[n], y_scales_i[:, :, lo * SCALE_INTS : hi * SCALE_INTS])

        def load_y(g, passes):
            source = y_words_i[passes, :, CODE_INTS * g : CODE_INTS * (g + 1)]
            nc.sync.dma_start(out=y_raw[g][:, passes, :], in_=source.rearrange("k p w -> p k w"))

        def load_v(passes):
            nc.sync.dma_start(out=v_codes[:, passes, :].bitcast(I32), in_=v_words_i[passes].rearrange("k p w -> p k w"))

        def load_u(g):
            rows = u[K_PASS * g : K_PASS * (g + 1), :].rearrange("(a t r) c -> r a t c", t=SLOTS, r=RUN)
            for r in range(RUN):
                nc.sync.dma_start(out=u_rows[g][r:P:RUN, :, :], in_=rows[r])

        def sort_y_scales(g):
            n = [i for i, (lo, hi) in enumerate(SCALE_RANGES) if lo <= g < hi][0]
            at = (g - SCALE_RANGES[n][0]) * SCALE_INTS
            nc.vector.tensor_copy(
                out=y_plane[g][:].bitcast(I32).rearrange("p k t (b i) -> p k b t i", i=NEAR),
                in_=y_scale_raw[n][:, :, at : at + SCALE_INTS].rearrange("p k (b i t) -> p k b t i", i=NEAR, t=SLOTS),
            )

        def sort_y_codes(g, passes):
            nc.vector.tensor_copy(
                out=y_codes[g][:, passes, :, :].bitcast(I32).rearrange("p k t (a w) -> p k t a w", w=2),
                in_=y_raw[g][:, passes, :].rearrange("p k (a t w) -> p k t a w", t=SLOTS, w=2),
            )

        def interleave(copy, mixed, rows, lo, hi):
            copy(
                out=mixed[:, lo:hi, :].rearrange("p (c i) t -> p c t i", i=NEAR),
                in_=rows[:, :, lo:hi].rearrange("p t (c i) -> p c t i", i=NEAR),
            )

        def quantize(codes, plane, mixed):
            nc.vector.quantize_mx(out=codes[:].bitcast(FP8X4), scales=plane[:], in_=mixed[:].rearrange("p c t -> p (c t)"))

        def quantize_u(g):
            quantize(u_codes[g], u_plane[g], u_mixed[g])

        def quantize_h(g):
            quantize(h_codes[g], h_plane[g], h_mixed[g])

        def stage_1_pass(acc, g, t, k):
            nc.tensor.matmul_mx(
                out=acc[:],
                lhsT=y_codes[g][:, k, t, :].bitcast(FP4X4),
                lhsT_scale=y_plane[g][:, k, t, :],
                rhs=v_codes[:, k, :].bitcast(FP4X4),
                rhs_scale=v_plane[:, k, :],
                start=(k == 0),
                stop=(k == TIME_PASSES - 1),
            )

        def stage_1(g, t):
            acc = first_acc[t] if g == 0 else bank((SLOTS * g + t) % ROTATING, [P, R])
            for k in range(1 if g == 0 else 0, TIME_PASSES):
                stage_1_pass(acc, g, t, k)
            nc.vector.scalar_tensor_tensor(
                out=h_rows[g][:, t, :], in0=acc[:], scalar=vol_col[:, t, g : g + 1], in1=sigma_inv_row[:], op0=MULT, op1=MULT
            )

        def stage_2(acc, g, m, columns):
            rows = slice(P * m, P * (m + 1))
            nc.tensor.matmul_mx(
                out=acc[:],
                lhsT=u_codes[g][:, rows].bitcast(FP8X4),
                lhsT_scale=u_plane[g][:, rows],
                rhs=h_codes[g][:, columns].bitcast(FP8X4),
                rhs_scale=h_plane[g][:, columns],
                start=(g == 0),
                stop=(g == LAST),
            )

        def store(copy, acc, m, columns):
            result = sbuf("result%d_%d" % (m, columns.start), [P, columns.stop - columns.start], F32)
            copy(out=result[:], in_=acc[:])
            nc.sync.dma_start(out=out[P * m : P * (m + 1), columns], in_=result[:])

        make_identity(nc, ident[:])
        v_plane_i = v_plane[:].bitcast(I32)
        nc.vector.memset(y_scale_raw[0][:], 0)
        nc.vector.memset(v_plane_i, 0)
        nc.vector.memset(vol_rows[:], 0.0)
        nc.vector.memset(y_scale_raw[1][:], 0)

        nc.scalar.dma_start(out=sigma_sb[:], in_=sigma.rearrange("(p m) -> p m", m=R // P))
        vol_by_group = vol.rearrange("(g c) -> g c", c=K_PASS)
        for groups in (slice(0, 4), slice(4, GROUPS)):
            nc.scalar.dma_start(out=vol_sb[groups, :], in_=vol_by_group[groups, :])
        load_y(0, first_pass)
        load_v(first_pass)
        load_y_scales(0)
        load_scale_rows(v_plane_i, v_scales_i)
        load_y(0, later_passes)
        load_v(later_passes)
        load_u(0)
        load_y_scales(1)
        for passes in pass_pairs:
            load_y(1, passes)
        load_u(1)

        nc.vector.reciprocal(out=sigma_inv[:], in_=sigma_sb[:])
        nc.vector.tensor_copy(
            out=vol_rows[0:GROUPS, :, :].rearrange("g t (a r) -> g t a r", r=RUN),
            in_=vol_sb[:].rearrange("g (a t r) -> g t a r", t=SLOTS, r=RUN),
        )
        sigma_ps = bank(ROTATING, [P, R // P, P])
        for m in range(R // P):
            nc.tensor.transpose(sigma_ps[:, m, :], sigma_inv[:, m : m + 1].to_broadcast([P, P]), ident[:])
        vol_ps = bank(ROTATING + 1, [P, SLOTS, P])
        for t in range(SLOTS):
            nc.tensor.transpose(vol_ps[:, t, :], vol_rows[:, t, :], ident[:])
        nc.scalar.copy(out=sigma_inv_row[:].rearrange("p (n m) -> p n m", n=P), in_=sigma_ps[:].rearrange("p m n -> p n m"))
        nc.scalar.copy(out=vol_col[:], in_=vol_ps[:, :, 0:GROUPS])
        wide_acc = [bank(ROTATING + m, [P, R]) for m in range(WIDE_TILES)]

        sort_y_codes(0, first_pass)
        sort_y_scales(0)
        first_acc = [bank(t, [P, R]) for t in range(SLOTS)]
        for t in range(SLOTS):
            stage_1_pass(first_acc[t], 0, t, 0)
        sort_y_codes(0, slice(1, 2))
        sort_y_codes(0, pass_pairs[1])

        for n in range(2, len(SCALE_RANGES)):
            nc.vector.memset(y_scale_raw[n][:], 0)
        load_y_scales(2)
        load_y(2, all_passes)
        load_u(2)
        load_y(3, all_passes)
        load_y_scales(3)
        load_u(3)
        for g in range(4, GROUPS):
            load_y(g, all_passes)
            load_u(g)

        interleave(nc.scalar.copy, u_mixed[0], u_rows[0], 0, R)
        for g in range(GROUPS):
            if g > 0:
                interleave(nc.scalar.copy, h_mixed[g - 1], h_rows[g - 1], 0, R)
            if g < LAST:
                interleave(nc.scalar.copy, u_mixed[g + 1], u_rows[g + 1], 0, R)
            stage_1(g, 0)
            if g >= LAG:
                quantize_h(g - LAG)
            stage_1(g, 1)
            if g == LAST:
                quantize_u(g)
                stage_1(g, 2)
            else:
                sort_y_scales(g + 1)
                for passes in pass_pairs if g == 0 else [all_passes]:
                    sort_y_codes(g + 1, passes)
                stage_1(g, 2)
                quantize_u(g)
            stage_1(g, 3)
            if 0 <= g - LAG < WOVEN:
                for m in range(WIDE_TILES):
                    stage_2(wide_acc[m], g - LAG, m, all_columns)

        quantize_h(LAST - 1)
        interleave(nc.vector.tensor_copy, h_mixed[LAST], h_rows[LAST], 0, H_SHARE)
        interleave(nc.scalar.copy, h_mixed[LAST], h_rows[LAST], H_SHARE, R)
        quantize_h(LAST)

        half_acc = [bank((SLOTS * GROUPS + n) % ROTATING, [P, R // 2]) for n in range(2)]
        for g in range(WOVEN, LAST - 1):
            for m in range(WIDE_TILES):
                stage_2(wide_acc[m], g, m, all_columns)
        for g in range(LAST):
            for n in range(2):
                stage_2(half_acc[n], g, WIDE_TILES, halves[n])
        for m in range(WIDE_TILES):
            stage_2(wide_acc[m], LAST - 1, m, all_columns)

        copies = (nc.scalar.copy, nc.vector.tensor_copy)
        for n in range(2):
            stage_2(half_acc[n], LAST, WIDE_TILES, halves[n])
            store(copies[n], half_acc[n], WIDE_TILES, halves[n])
        for m in range(WIDE_TILES):
            stage_2(wide_acc[m], LAST, m, all_columns)
            store(copies[m % 2], wide_acc[m], m, all_columns)
